import numpy as np, ml_dtypes
CORES = [21,85,149,213,277,341,405,469]
N = 8
F = 256
def setup_inputs(rng):
    return {"a": rng.standard_normal((N, 128, 128), dtype=np.float32).astype(ml_dtypes.bfloat16), "w": rng.standard_normal((N, 128, F), dtype=np.float32).astype(ml_dtypes.bfloat16)}
def setup_inputs_big(rng):
    d = setup_inputs(rng)
    for k in ("a", "w"): d[k] = (d[k].astype(np.float32) * 1024.0).astype(d[k].dtype)
    return d
def setup_inputs_small(rng):
    d = setup_inputs(rng)
    for k in ("a", "w"): d[k] = (d[k].astype(np.float32) * (1 / 1024.0)).astype(d[k].dtype)
    return d
def setup_inputs_apart(rng):
    d = setup_inputs(rng)
    f = (10.0 ** rng.permutation(np.linspace(-1.5, 1.5, N))).astype(np.float32).reshape(N, 1, 1)
    for k in ("a", "w"): d[k] = (d[k].astype(np.float32) * f).astype(d[k].dtype)
    return d
def reference(a, w):
    A, W = a.astype(np.float64), w.astype(np.float64)
    p = np.stack([A[j].T @ W[j] for j in range(N)])
    return {"y": np.cumsum(p, axis=0).astype(ml_dtypes.bfloat16 if a.dtype != np.float64 else np.float64)}

@@ -1,0 +1,106 @@
+from concourse.bass import DstId, RemoteDMATransfer
+from concourse.mybir import AluOpType
+
+F = 256
+SCRATCH = {
+    "a_sb": ("sbuf", [128, 128], "bfloat16"),
+    "w_sb": ("sbuf", [128, F], "bfloat16"),
+    "acc": ("psum", [128, F], "float32"),
+    "p_sb": ("sbuf", [128, F], "bfloat16"),
+    "land0": ("sbuf", [128, F], "bfloat16"),
+    "land1": ("sbuf", [128, F], "bfloat16"),
+    "land2": ("sbuf", [128, F], "bfloat16"),
+    "land3": ("sbuf", [128, F], "bfloat16"),
+    "base": ("sbuf", [128, F], "bfloat16"),
+    "y_sb": ("sbuf", [128, F], "bfloat16"),
+}
+SEMAPHORES = ["loaded", "mm", "cp", "arr", "cab", "sent", "vs", "ydone", "stored"]
+
+
+def _engines(mask):
+    return sum(1 for b in range(16) if (mask >> b) & 1)
+
+
+def rank_program(g, core, T, topo):
+    rank = T.rank_of(core)
+    if rank is None:
+        return
+    S = T.sem
+
+    def rack_of(c):
+        return topo.rack(topo.host(c))
+
+    mine = [c for c in T.cores if rack_of(c) == rack_of(core)]
+    other = [c for c in T.cores if rack_of(c) != rack_of(core)]
+    q = mine.index(core)
+    first = rack_of(core) == rack_of(T.cores[0])
+    for c in mine:
+        assert c == core or topo.same_plane(core, c)
+
+    g.sync.dma_start(T.w_sb[:], T.w[:]).then_inc(S.loaded, 16)
+    g.scalar.dma_start(T.a_sb[:], T.a[:]).then_inc(S.loaded, 16)
+    g.tensor.wait_ge(S.loaded, 32)
+    g.tensor.matmul(T.acc[:], T.a_sb[:], T.w_sb[:], True, True).then_inc(S.mm, 1)
+    g.vector.wait_ge(S.mm, 1)
+    g.vector.tensor_copy(T.p_sb[:], T.acc[:]).then_inc(S.cp, 1)
+
+    dests = [c for c in mine if c != core] if first else mine[q + 1:]
+    n_in = (len(mine) - 1) if first else q
+    sent = 0
+    g.wait_ge(S.cp, 1)
+    if dests:
+        m = topo.mask(core, dests[0])
+        for d in dests:
+            m &= topo.mask(core, d)
+        ids = []
+        for d in dests:
+            rid, pid = topo.addr(d, core)
+            ids.append(DstId(rid=rid, pnc=pid))
+        g.remote_dma_fused([RemoteDMATransfer(
+            dst_ids=ids, dma_engine_mask=m, remote_sem=S.arr,
+            srcs=[T.p_sb[:]], dsts=[T["land%d" % q][:] for _ in dests], alu_op=0)], local_sem=S.sent)
+        sent += _engines(m)
+    per = _engines(topo.mask(core, mine[(q + 1) % len(mine)]))
+
+    if first:
+        far = [d for d in other if topo.may_write(core, d) and topo.chip(d) == topo.chip(core)]
+        assert len(far) == 1
+        d = far[0]
+        rid, pid = topo.addr(d, core)
+        m = topo.mask(core, d)
+        g.wait_ge(S.arr, per * n_in)
+        srcs = [T.p_sb[:] if k == q else T["land%d" % k][:] for k in range(len(mine))]
+        g.remote_dma_fused([RemoteDMATransfer(
+            dst_ids=[DstId(rid=rid, pnc=pid)], dma_engine_mask=m, remote_sem=S.cab,
+            srcs=srcs, dsts=[T.base[:]], alu_op=1)], local_sem=S.sent)
+        sent += _engines(m)
+    if sent:
+        g.wait_ge(S.sent, sent)
+
+    terms = [T["land%d" % k] for k in range(q)]
+    if not first:
+        terms.append(T.base)
+    if not terms:
+        y_src = T.p_sb
+        g.sync.wait_ge(S.cp, 1)
+    else:
+        y_src = T.y_sb
+        g.vector.wait_ge(S.cp, 1)
+        if n_in:
+            g.vector.wait_ge(S.arr, per * n_in)
+        for i, t in enumerate(terms):
+            last = i == len(terms) - 1
+            if last and not first:
+                gate = [c for c in other if topo.may_write(c, core) and topo.chip(c) == topo.chip(core)]
+                g.vector.wait_ge(S.cab, _engines(topo.mask(gate[0], core)))
+            if i:
+                g.vector.wait_ge(S.vs, i)
+            if last:
+                g.vector.tensor_tensor(T.y_sb[:], T.acc[:], t[:], AluOpType.add).then_inc(S.ydone, 1)
+            else:
+                g.vector.tensor_tensor(T.acc[:], T.acc[:], t[:], AluOpType.add).then_inc(S.vs, 1)
+        g.sync.wait_ge(S.ydone, 1)
+    if first:
+        g.sync.wait_ge(S.sent, sent)
+    g.sync.dma_start(T.y[:], y_src[:]).then_inc(S.stored, 16)
+    g.sync.wait_ge(S.stored, 16)

@@ -1,20 +1,26 @@
 from concourse.bass import DstId, RemoteDMATransfer
 from concourse.mybir import AluOpType
 
+K = 128
 F = 256
 SCRATCH = {
-    "a_sb": ("sbuf", [128, 128], "bfloat16"),
-    "w_sb": ("sbuf", [128, F], "bfloat16"),
-    "acc": ("psum", [128, F], "float32"),
+    "aw": ("sbuf", [128, K + F], "bfloat16"),
+    "acc": ("psum", [128, 512], "float32"),
+    "acc2": ("psum", [128, 512], "float32"),
     "p_sb": ("sbuf", [128, F], "bfloat16"),
+    "pair": ("sbuf", [128, F], "bfloat16"),
     "land0": ("sbuf", [128, F], "bfloat16"),
     "land1": ("sbuf", [128, F], "bfloat16"),
     "land2": ("sbuf", [128, F], "bfloat16"),
     "land3": ("sbuf", [128, F], "bfloat16"),
+    "raw0": ("sbuf", [128, K + F], "bfloat16"),
+    "raw1": ("sbuf", [128, K + F], "bfloat16"),
+    "raw2": ("sbuf", [128, K + F], "bfloat16"),
+    "rawn": ("sbuf", [128, K + F], "bfloat16"),
     "base": ("sbuf", [128, F], "bfloat16"),
     "y_sb": ("sbuf", [128, F], "bfloat16"),
 }
-SEMAPHORES = ["loaded", "mm", "cp", "arr", "cab", "sent", "vs", "ydone", "stored"]
+SEMAPHORES = ["loaded", "mm", "mm2", "cp", "pr", "rawa", "arr", "cab", "sent", "vs", "ydone", "stored"]
 
 
 def _engines(mask):
@@ -30,77 +36,107 @@ def rank_program(g, core, T, topo):
     def rack_of(c):
         return topo.rack(topo.host(c))
 
-    mine = [c for c in T.cores if rack_of(c) == rack_of(core)]
-    other = [c for c in T.cores if rack_of(c) != rack_of(core)]
+    lead = [c for c in T.cores if rack_of(c) == rack_of(T.cores[0])]
+    tail = [c for c in T.cores if rack_of(c) != rack_of(T.cores[0])]
+    first = core in lead
+    mine = lead if first else tail
     q = mine.index(core)
-    first = rack_of(core) == rack_of(T.cores[0])
+    n = len(mine)
     for c in mine:
         assert c == core or topo.same_plane(core, c)
 
-    g.sync.dma_start(T.w_sb[:], T.w[:]).then_inc(S.loaded, 16)
-    g.scalar.dma_start(T.a_sb[:], T.a[:]).then_inc(S.loaded, 16)
-    g.tensor.wait_ge(S.loaded, 32)
-    g.tensor.matmul(T.acc[:], T.a_sb[:], T.w_sb[:], True, True).then_inc(S.mm, 1)
-    g.vector.wait_ge(S.mm, 1)
-    g.vector.tensor_copy(T.p_sb[:], T.acc[:]).then_inc(S.cp, 1)
+    def behind(c):
+        far = [d for d in tail if topo.may_write(c, d) and topo.chip(d) == topo.chip(c)]
+        assert len(far) == 1
+        return far[0]
 
-    dests = [c for c in mine if c != core] if first else mine[q + 1:]
-    n_in = (len(mine) - 1) if first else q
-    sent = 0
-    g.wait_ge(S.cp, 1)
-    if dests:
+    sent = [0]
+
+    def send(dests, srcs, out, sem, op):
         m = topo.mask(core, dests[0])
-        for d in dests:
-            m &= topo.mask(core, d)
         ids = []
         for d in dests:
+            m &= topo.mask(core, d)
             rid, pid = topo.addr(d, core)
             ids.append(DstId(rid=rid, pnc=pid))
         g.remote_dma_fused([RemoteDMATransfer(
-            dst_ids=ids, dma_engine_mask=m, remote_sem=S.arr,
-            srcs=[T.p_sb[:]], dsts=[T["land%d" % q][:] for _ in dests], alu_op=0)], local_sem=S.sent)
-        sent += _engines(m)
-    per = _engines(topo.mask(core, mine[(q + 1) % len(mine)]))
+            dst_ids=ids, dma_engine_mask=m, remote_sem=sem,
+            srcs=srcs, dsts=[out[:] for _ in dests], alu_op=op)], local_sem=S.sent)
+        sent[0] += _engines(m)
+
+    def lands(src):
+        return _engines(topo.mask(src, core))
+
+    own_a, own_w = T.aw[:, 0:K], T.aw[:, K:K + F]
+    A1, A2 = T.acc[:, 0:F], T.acc2[:, 0:F]
+
+    g.sync.dma_start(own_w, T.w[:]).then_inc(S.loaded, 16)
+    g.scalar.dma_start(own_a, T.a[:]).then_inc(S.loaded, 16)
+    g.tensor.wait_ge(S.loaded, 32)
 
     if first:
-        far = [d for d in other if topo.may_write(core, d) and topo.chip(d) == topo.chip(core)]
-        assert len(far) == 1
-        d = far[0]
-        rid, pid = topo.addr(d, core)
-        m = topo.mask(core, d)
-        g.wait_ge(S.arr, per * n_in)
-        srcs = [T.p_sb[:] if k == q else T["land%d" % k][:] for k in range(len(mine))]
-        g.remote_dma_fused([RemoteDMATransfer(
-            dst_ids=[DstId(rid=rid, pnc=pid)], dma_engine_mask=m, remote_sem=S.cab,
-            srcs=srcs, dsts=[T.base[:]], alu_op=1)], local_sem=S.sent)
-        sent += _engines(m)
-    if sent:
-        g.wait_ge(S.sent, sent)
+        nxt = mine[(q + 1) % n]
+        rest = [mine[(q + i) % n] for i in range(2, n)]
+        prev = mine[(q - 1) % n]
+        givers = [c for c in mine if c != core and c != prev]
 
-    terms = [T["land%d" % k] for k in range(q)]
-    if not first:
-        terms.append(T.base)
-    if not terms:
-        y_src = T.p_sb
-        g.sync.wait_ge(S.cp, 1)
+        g.wait_ge(S.loaded, 32)
+        send([nxt], [T.aw[:]], T.rawn, S.rawa, 0)
+        g.wait_ge(S.cp, 1)
+        send(rest, [T.p_sb[:]], T["land%d" % q], S.arr, 0)
+        n_arr = sum(lands(c) for c in givers)
+        g.wait_ge(S.arr, n_arr)
+        g.wait_ge(S.pr, 1)
+        send([behind(core)], [T.pair[:]] + [T["land%d" % mine.index(c)][:] for c in givers], T.base, S.cab, 1)
+        g.wait_ge(S.sent, sent[0])
+
+        g.tensor.matmul(A1, own_a, own_w, True, True).then_inc(S.mm, 1)
+        g.tensor.matmul(A2, own_a, own_w, True, False)
+        g.tensor.wait_ge(S.rawa, lands(prev))
+        g.tensor.matmul(A2, T.rawn[:, 0:K], T.rawn[:, K:K + F], False, True).then_inc(S.mm2, 1)
+
+        g.vector.wait_ge(S.mm, 1)
+        g.vector.tensor_copy(T.p_sb[:], A1).then_inc(S.cp, 1)
+        g.vector.wait_ge(S.mm2, 1)
+        g.vector.tensor_copy(T.pair[:], A2).then_inc(S.pr, 1)
+        terms = [T["land%d" % k] for k in range(q - 1)]
+        if q == 0:
+            y_src = T.p_sb
+            g.sync.wait_ge(S.cp, 1)
+        elif not terms:
+            y_src = T.pair
+            g.sync.wait_ge(S.pr, 1)
+        else:
+            y_src = T.y_sb
+            g.vector.wait_ge(S.pr, 1)
+            g.vector.wait_ge(S.arr, n_arr)
+            for i, t in enumerate(terms):
+                if i:
+                    g.vector.wait_ge(S.vs, i)
+                if i == len(terms) - 1:
+                    g.vector.tensor_tensor(T.y_sb[:], A2, t[:], AluOpType.add).then_inc(S.ydone, 1)
+                else:
+                    g.vector.tensor_tensor(A2, A2, t[:], AluOpType.add).then_inc(S.vs, 1)
+            g.sync.wait_ge(S.ydone, 1)
+        g.sync.wait_ge(S.sent, sent[0])
     else:
+        if mine[q + 1:]:
+            g.wait_ge(S.loaded, 32)
+            send(mine[q + 1:], [T.aw[:]], T["raw%d" % q], S.arr, 0)
+            g.wait_ge(S.sent, sent[0])
+        g.tensor.matmul(A1, own_a, own_w, True, q == 0).then_inc(S.mm, 1)
+        if q:
+            g.tensor.wait_ge(S.arr, sum(lands(c) for c in mine[:q]))
+        for k in range(q):
+            r = T["raw%d" % k]
+            g.tensor.matmul(A1, r[:, 0:K], r[:, K:K + F], False, k == q - 1).then_inc(S.mm, 1)
+
+        gate = [c for c in lead if behind(c) == core][0]
+        g.vector.wait_ge(S.mm, q + 1)
+        g.vector.wait_ge(S.cab, lands(gate))
+        g.vector.tensor_tensor(T.y_sb[:], A1, T.base[:], AluOpType.add).then_inc(S.ydone, 1)
         y_src = T.y_sb
-        g.vector.wait_ge(S.cp, 1)
-        if n_in:
-            g.vector.wait_ge(S.arr, per * n_in)
-        for i, t in enumerate(terms):
-            last = i == len(terms) - 1
-            if last and not first:
-                gate = [c for c in other if topo.may_write(c, core) and topo.chip(c) == topo.chip(core)]
-                g.vector.wait_ge(S.cab, _engines(topo.mask(gate[0], core)))
-            if i:
-                g.vector.wait_ge(S.vs, i)
-            if last:
-                g.vector.tensor_tensor(T.y_sb[:], T.acc[:], t[:], AluOpType.add).then_inc(S.ydone, 1)
-            else:
-                g.vector.tensor_tensor(T.acc[:], T.acc[:], t[:], AluOpType.add).then_inc(S.vs, 1)
         g.sync.wait_ge(S.ydone, 1)
-    if first:
-        g.sync.wait_ge(S.sent, sent)
+
     g.sync.dma_start(T.y[:], y_src[:]).then_inc(S.stored, 16)
     g.sync.wait_ge(S.stored, 16)

from concourse.bass import DstId, RemoteDMATransfer
from concourse.mybir import AluOpType

K = 128
F = 256
SCRATCH = {
    "aw": ("sbuf", [128, K + F], "bfloat16"),
    "acc": ("psum", [128, 512], "float32"),
    "acc2": ("psum", [128, 512], "float32"),
    "p_sb": ("sbuf", [128, F], "bfloat16"),
    "pair": ("sbuf", [128, F], "bfloat16"),
    "land0": ("sbuf", [128, F], "bfloat16"),
    "land1": ("sbuf", [128, F], "bfloat16"),
    "land2": ("sbuf", [128, F], "bfloat16"),
    "land3": ("sbuf", [128, F], "bfloat16"),
    "raw0": ("sbuf", [128, K + F], "bfloat16"),
    "raw1": ("sbuf", [128, K + F], "bfloat16"),
    "raw2": ("sbuf", [128, K + F], "bfloat16"),
    "rawn": ("sbuf", [128, K + F], "bfloat16"),
    "base": ("sbuf", [128, F], "bfloat16"),
    "y_sb": ("sbuf", [128, F], "bfloat16"),
}
SEMAPHORES = ["loaded", "mm", "mm2", "cp", "pr", "rawa", "arr", "cab", "sent", "vs", "ydone", "stored"]


def _engines(mask):
    return sum(1 for b in range(16) if (mask >> b) & 1)


def rank_program(g, core, T, topo):
    rank = T.rank_of(core)
    if rank is None:
        return
    S = T.sem

    def rack_of(c):
        return topo.rack(topo.host(c))

    lead = [c for c in T.cores if rack_of(c) == rack_of(T.cores[0])]
    tail = [c for c in T.cores if rack_of(c) != rack_of(T.cores[0])]
    first = core in lead
    mine = lead if first else tail
    q = mine.index(core)
    n = len(mine)
    for c in mine:
        assert c == core or topo.same_plane(core, c)

    def behind(c):
        far = [d for d in tail if topo.may_write(c, d) and topo.chip(d) == topo.chip(c)]
        assert len(far) == 1
        return far[0]

    sent = [0]

    def send(dests, srcs, out, sem, op):
        m = topo.mask(core, dests[0])
        ids = []
        for d in dests:
            m &= topo.mask(core, d)
            rid, pid = topo.addr(d, core)
            ids.append(DstId(rid=rid, pnc=pid))
        g.remote_dma_fused([RemoteDMATransfer(
            dst_ids=ids, dma_engine_mask=m, remote_sem=sem,
            srcs=srcs, dsts=[out[:] for _ in dests], alu_op=op)], local_sem=S.sent)
        sent[0] += _engines(m)

    def lands(src):
        return _engines(topo.mask(src, core))

    own_a, own_w = T.aw[:, 0:K], T.aw[:, K:K + F]
    A1, A2 = T.acc[:, 0:F], T.acc2[:, 0:F]

    g.sync.dma_start(own_w, T.w[:]).then_inc(S.loaded, 16)
    g.scalar.dma_start(own_a, T.a[:]).then_inc(S.loaded, 16)
    g.tensor.wait_ge(S.loaded, 32)

    if first:
        nxt = mine[(q + 1) % n]
        rest = [mine[(q + i) % n] for i in range(2, n)]
        prev = mine[(q - 1) % n]
        givers = [c for c in mine if c != core and c != prev]

        g.wait_ge(S.loaded, 32)
        send([nxt], [T.aw[:]], T.rawn, S.rawa, 0)
        g.wait_ge(S.cp, 1)
        send(rest, [T.p_sb[:]], T["land%d" % q], S.arr, 0)
        n_arr = sum(lands(c) for c in givers)
        g.wait_ge(S.arr, n_arr)
        g.wait_ge(S.pr, 1)
        send([behind(core)], [T.pair[:]] + [T["land%d" % mine.index(c)][:] for c in givers], T.base, S.cab, 1)
        g.wait_ge(S.sent, sent[0])

        g.tensor.matmul(A1, own_a, own_w, True, True).then_inc(S.mm, 1)
        g.tensor.matmul(A2, own_a, own_w, True, False)
        g.tensor.wait_ge(S.rawa, lands(prev))
        g.tensor.matmul(A2, T.rawn[:, 0:K], T.rawn[:, K:K + F], False, True).then_inc(S.mm2, 1)

        g.vector.wait_ge(S.mm, 1)
        g.vector.tensor_copy(T.p_sb[:], A1).then_inc(S.cp, 1)
        g.vector.wait_ge(S.mm2, 1)
        g.vector.tensor_copy(T.pair[:], A2).then_inc(S.pr, 1)
        terms = [T["land%d" % k] for k in range(q - 1)]
        if q == 0:
            y_src = T.p_sb
            g.sync.wait_ge(S.cp, 1)
        elif not terms:
            y_src = T.pair
            g.sync.wait_ge(S.pr, 1)
        else:
            y_src = T.y_sb
            g.vector.wait_ge(S.pr, 1)
            g.vector.wait_ge(S.arr, n_arr)
            for i, t in enumerate(terms):
                if i:
                    g.vector.wait_ge(S.vs, i)
                if i == len(terms) - 1:
                    g.vector.tensor_tensor(T.y_sb[:], A2, t[:], AluOpType.add).then_inc(S.ydone, 1)
                else:
                    g.vector.tensor_tensor(A2, A2, t[:], AluOpType.add).then_inc(S.vs, 1)
            g.sync.wait_ge(S.ydone, 1)
        g.sync.wait_ge(S.sent, sent[0])
    else:
        if mine[q + 1:]:
            g.wait_ge(S.loaded, 32)
            send(mine[q + 1:], [T.aw[:]], T["raw%d" % q], S.arr, 0)
            g.wait_ge(S.sent, sent[0])
        g.tensor.matmul(A1, own_a, own_w, True, q == 0).then_inc(S.mm, 1)
        if q:
            g.tensor.wait_ge(S.arr, sum(lands(c) for c in mine[:q]))
        for k in range(q):
            r = T["raw%d" % k]
            g.tensor.matmul(A1, r[:, 0:K], r[:, K:K + F], False, k == q - 1).then_inc(S.mm, 1)

        gate = [c for c in lead if behind(c) == core][0]
        g.vector.wait_ge(S.mm, q + 1)
        g.vector.wait_ge(S.cab, lands(gate))
        g.vector.tensor_tensor(T.y_sb[:], A1, T.base[:], AluOpType.add).then_inc(S.ydone, 1)
        y_src = T.y_sb
        g.sync.wait_ge(S.ydone, 1)

    g.sync.dma_start(T.y[:], y_src[:]).then_inc(S.stored, 16)
    g.sync.wait_ge(S.stored, 16)
